import numpy as np
import ml_dtypes


def mxq(x, axis, fmt="e4m3"):
    dtype, down = {"e4m3": (ml_dtypes.float8_e4m3fn, 7), "e5m2": (ml_dtypes.float8_e5m2, 14)}[fmt]
    v = np.moveaxis(np.asarray(x, np.float32).astype(ml_dtypes.bfloat16).astype(np.float64), axis, -1)
    blocks = v.reshape(v.shape[:-1] + (-1, 32))
    amax = np.abs(blocks).max(-1, keepdims=True)
    byte = np.maximum(np.where(amax > 0, np.frexp(amax)[1] - 1 + 127, 0) - down, 1)
    scale = np.exp2(byte - 127.0)
    codes = (blocks / scale).astype(np.float32).astype(dtype).astype(np.float64)
    return np.moveaxis((codes * scale).reshape(v.shape), -1, axis)


WIDE = False


def mx_kscale(k):
    if not WIDE:
        return np.ones(k)
    levels = np.array([10, -10, 5, -5, 0])
    if k % 512:
        return np.exp2(np.random.permutation(np.resize(levels, k // 32))).repeat(32)
    a = np.empty((k // 512, 16))
    for p in range(k // 512):
        a[p, :8] = np.random.permutation(np.resize(levels, 8))
        for g in range(8):
            far = levels[np.abs(levels - a[p, g]) >= 10]
            a[p, g + 8] = far[np.random.randint(len(far))]
    return np.exp2(a.ravel()).repeat(32)


def f64(x):
    return np.asarray(x).astype(np.float64)


def striped(idx):
    return np.tile(idx.reshape(-1, 16).T, (8, 1)).astype(np.uint16)


def unstriped(offs):
    return offs[:16].T.reshape(-1).astype(np.int64)


E2M1 = np.array([0.0, 0.5, 1.0, 1.5, 2.0, 3.0, 4.0, 6.0, -0.0, -0.5, -1.0, -1.5, -2.0, -3.0, -4.0, -6.0])


def pack_weight(w, fmt):
    k, n = w.shape
    w = f64(np.asarray(w, np.float32).astype(ml_dtypes.bfloat16)).reshape(k // 32, 32, n)
    amax = np.abs(w).max(1)
    if fmt == "e4m3":
        byte = np.frexp(amax)[1] - 1 + 127 - 7
    else:
        mant, ex = np.frexp(amax / 6.0)
        byte = np.where(mant > 0.5, ex, ex - 1) + 127
    byte = np.clip(np.where(amax > 0, byte, 1), 1, 254)
    scaled = (w * np.exp2(127.0 - byte)[:, None, :]).reshape(k, n).astype(np.float32)
    by_word = np.ascontiguousarray(scaled.reshape(k // 512, 128, 4, n).transpose(0, 1, 3, 2))
    if fmt == "e4m3":
        words = by_word.astype(ml_dtypes.float8_e4m3fn).view(np.uint8)
    else:
        c = by_word.astype(ml_dtypes.float4_e2m1fn).view(np.uint8) & 0xF
        words = (c[..., 0::2] | (c[..., 1::2] << 4)).reshape(k // 512, 128, 2 * n)
    return np.ascontiguousarray(words), np.ascontiguousarray(byte.astype(np.uint8).reshape(k // 512, 16, n))


def unpack_weight(words, scales, fmt):
    g, _, n = scales.shape
    words = np.ascontiguousarray(words).reshape(g, 128, n, -1)
    if fmt == "e4m3":
        vals = words.view(ml_dtypes.float8_e4m3fn).astype(np.float64)
    else:
        nib = np.empty((g, 128, n, 4), np.uint8)
        nib[..., 0::2] = words & 0xF
        nib[..., 1::2] = words >> 4
        vals = E2M1[nib]
    vals = vals * np.repeat(np.exp2(scales.astype(np.float64) - 127.0), 8, axis=1)[..., None]
    return vals.transpose(0, 1, 3, 2).reshape(g * 512, n)


def gelu(v):
    return 0.5 * v * (1.0 + np.tanh(np.sqrt(2.0 / np.pi) * (v + 0.044715 * v**3)))


def twice(P):
    return np.random.permutation(np.repeat(np.arange(P), 2))


K, H, T, S, P = 1024, 1024, 4096, 1024, 512

def setup_inputs():
    n = np.random.standard_normal
    s = mx_kscale(K)[:, None]
    u = mx_kscale(H)[:, None]
    d = {}
    d["tab_words"], d["tab_scales"] = pack_weight(n((K, T)) * s, "e4m3")
    d["offs"] = striped(np.random.permutation(T)[:S])
    perm = np.random.permutation(S)
    d["pos1"] = striped(perm[:P])
    d["pos2"] = striped(perm[-P:])
    d["pos3"] = striped(twice(P))
    d["w1"] = (n((K, H)) / K**0.5 / s * u.T).astype(np.float32)
    d["wn_words"], d["wn_scales"] = pack_weight(1.5 * n((H, H)) / H**0.5 / u, "e2m1")
    d["wd"] = (n((H, H)) / H**0.5 / u).astype(np.float32)
    d["bd"] = (0.8 * n(H)).astype(np.float32)
    d["gain"] = (0.8 * np.exp(0.4 * n(H)) / u[:, 0]).astype(np.float32)
    return d

def reference(tab_words, tab_scales, offs, pos1, pos2, pos3, w1, wn_words, wn_scales, wd, bd, gain):
    v = unpack_weight(tab_words, tab_scales, "e4m3")[:, unstriped(offs)]
    h = mxq(f64(w1), 0, "e4m3").T @ v
    x = h[:, unstriped(pos1)] - h[:, unstriped(pos2)]
    xq = mxq(x, 0, "e4m3")
    num = unpack_weight(wn_words, wn_scales, "e2m1").T @ xq
    den = mxq(f64(wd), 0, "e4m3").T @ xq
    y = num / (1.0 + np.abs(den + f64(bd)[:, None]))
    out = y[:, unstriped(pos3)] + f64(gain)[:, None] * h
    return out

@@ -1,0 +1,332 @@
+from contextlib import ExitStack
+
+import concourse.mybir as mybir
+
+K, H, T, S, L = 1024, 1024, 4096, 1024, 512
+FLOPS = 2 * K * H * S + 2 * 2 * H * H * L
+
+F32 = mybir.dt.float32
+BF16 = mybir.dt.bfloat16
+I32 = mybir.dt.int32
+U32 = mybir.dt.uint32
+U16 = mybir.dt.uint16
+U8 = mybir.dt.uint8
+FP8X4 = mybir.dt.float8_e4m3fn_x4
+FP4X4 = mybir.dt.float4_e2m1fn_x4
+ACT = mybir.ActivationFunctionType
+ALU = mybir.AluOpType
+
+P = 128
+PACK = 4
+KP = P * PACK
+PASSES = 2
+BANK = 512
+HALF = L // 2
+BACK = 256
+
+
+def tile_list_longline_buoy_biomass_kernel(
+    tc, tab_words, tab_scales, offs, pos1, pos2, pos3, w1, wn_words, wn_scales, wd, bd, gain, out
+):
+    nc = tc.nc
+    with ExitStack() as ctx:
+        keep = ctx.enter_context(tc.tile_pool(name="keep", bufs=1))
+        ring = ctx.enter_context(tc.tile_pool(name="ring", bufs=2))
+        psum = ctx.enter_context(tc.psum_pool(name="psum", bufs=8))
+
+        offs_sb = keep.tile([P, S // 16], U16, name="offs_sb")
+        pos1_sb = keep.tile([P, L // 16], U16, name="pos1_sb")
+        pos2_sb = keep.tile([P, L // 16], U16, name="pos2_sb")
+        pos3_sb = keep.tile([P, S // 16], U16, name="pos3_sb")
+        bd_sb = keep.tile([P, PASSES, PACK], F32, name="bd_sb")
+        gain_sb = keep.tile([P, PASSES, PACK], F32, name="gain_sb")
+
+        tab_sc = keep.tile([P, T], U8, name="tab_sc", align_bytes=64)
+        wn_sc_raw = keep.tile([P, PASSES * H], U8, name="wn_sc_raw", align_bytes=64)
+        wn_raw = keep.tile([P, PASSES * 2 * H], U8, name="wn_raw", align_bytes=64)
+        nc.vector.memset(wn_sc_raw[:].bitcast(I32), 0)
+        nc.gpsimd.memset(tab_sc[:].bitcast(I32), 0)
+
+        def load_weight(w, a, b):
+            raw = ring.tile([P, PACK, KP], F32, name="w_raw", bufs=5)
+            nc.sync.dma_start(
+                out=raw[:],
+                in_=w[a * KP : (a + 1) * KP, b * KP : (b + 1) * KP].rearrange("(p j) c -> p j c", j=PACK),
+            )
+            return raw
+
+        def load_table(a):
+            words = ring.tile([P, T], U32, name="tab_w", tag="wide", align_bytes=64)
+            nc.sync.dma_start(
+                out=words[:].bitcast(I32), in_=tab_words[a].rearrange("p t i -> p (t i)").bitcast(I32)
+            )
+            return words
+
+        def load_table_scales(a):
+            for q in range(4):
+                nc.sync.dma_start(
+                    out=tab_sc[32 * q + 4 * a : 32 * q + 4 * a + 4, :].bitcast(I32),
+                    in_=tab_scales[a, 4 * q : 4 * q + 4, :].bitcast(I32),
+                )
+
+        nc.sync.dma_start(
+            out=wn_raw[:].bitcast(I32).rearrange("p (a c) -> p a c", a=PASSES),
+            in_=wn_words.bitcast(I32).rearrange("a p c -> p a c"),
+        )
+        for q in range(4):
+            nc.sync.dma_start(
+                out=wn_sc_raw[32 * q : 32 * q + 4, :].bitcast(I32).rearrange("r (a c) -> r a c", a=PASSES),
+                in_=wn_scales[:, 4 * q : 4 * q + 4, :].bitcast(I32).rearrange("a r c -> r a c"),
+            )
+        tab_w = [load_table(0)]
+        nc.sync.dma_start(offs_sb[:], offs)
+        load_table_scales(0)
+        w1_raw = {}
+        w1_raw[0, 0] = load_weight(w1, 0, 0)
+        load_table_scales(1)
+        tab_w.append(load_table(1))
+        w1_raw[1, 0] = load_weight(w1, 1, 0)
+        nc.sync.dma_start(pos2_sb[:], pos2)
+        nc.sync.dma_start(pos1_sb[:], pos1)
+        for a in range(PASSES):
+            w1_raw[a, 1] = load_weight(w1, a, 1)
+        nc.sync.dma_start(pos3_sb[:], pos3)
+        nc.sync.dma_start(out=bd_sb[:], in_=bd.rearrange("(b p t) -> p b t", b=PASSES, t=PACK))
+        nc.sync.dma_start(out=gain_sb[:], in_=gain.rearrange("(b p t) -> p b t", b=PASSES, t=PACK))
+        wd_raw = {(a, b): load_weight(wd, a, b) for b in range(PASSES) for a in range(PASSES)}
+
+        def quantize(woven, name):
+            n = woven.shape[1] // PACK
+            codes = keep.tile([P, n], U32, name=name + "_codes", align_bytes=64)
+            scales = keep.tile([P, n], U8, name=name + "_scales", align_bytes=64)
+            nc.vector.quantize_mx(out=codes[:].bitcast(FP8X4), scales=scales[:], in_=woven[:])
+            return codes, scales
+
+        def weight_operands(raw, name, t0, t1, weave=nc.scalar.copy, tag="woven", bufs=3):
+            woven = ring.tile([P, (t1 - t0) * KP], BF16, name="woven", tag=tag, bufs=bufs, align_bytes=64)
+            weave(
+                out=woven[:].rearrange("p (t m j) -> p m j t", m=P, j=PACK),
+                in_=raw[:].rearrange("p j (m t) -> p m j t", t=PACK)[:, :, :, t0:t1],
+            )
+            codes, scales = quantize(woven, f"{name}_{t0}")
+            return [
+                (codes[:, t * P : (t + 1) * P].bitcast(FP8X4), scales[:, t * P : (t + 1) * P]) for t in range(t1 - t0)
+            ]
+
+        wn_w = keep.tile([P, PASSES * 2 * H], U8, name="wn_w", align_bytes=64)
+        wn_sc = keep.tile([P, PASSES * H], U8, name="wn_sc", align_bytes=64)
+        nc.vector.tensor_copy(
+            out=wn_w[:].bitcast(U16).rearrange("p (g t m) -> p g m t", t=PACK, m=P),
+            in_=wn_raw[:].bitcast(U16).rearrange("p (g m t) -> p g m t", t=PACK, m=P),
+        )
+        nc.vector.tensor_copy(
+            out=wn_sc[:].rearrange("p (g t m) -> p g m t", t=PACK, m=P),
+            in_=wn_sc_raw[:].rearrange("p (g m t) -> p g m t", t=PACK, m=P),
+        )
+
+        def pick_words(a):
+            picked = keep.tile([P, S], U32, name=f"v_w{a}", align_bytes=64)
+            nc.vector.tensor_copy(picked[:], tab_w[a][:].indirect(offs_sb[:]))
+            return picked
+
+        v_w = [pick_words(0)]
+        v_sc = keep.tile([P, S], U8, name="v_sc", align_bytes=64)
+        nc.vector.tensor_copy(v_sc[:], tab_sc[:].indirect(offs_sb[:]))
+        w1q = {}
+        w1q[0, 0] = weight_operands(w1_raw[0, 0], "w1_00", 0, 2) + weight_operands(w1_raw[0, 0], "w1_00", 2, 4)
+        v_w.append(pick_words(1))
+        w1q[1, 0] = weight_operands(w1_raw[1, 0], "w1_10", 0, 2)
+
+        h_sb = {}
+
+        def first_stage(b, t):
+            banks = [psum.tile([P, BANK], F32, name="bank") for c in range(S // BANK)]
+            for a in range(PASSES):
+                for c in range(S // BANK):
+                    cols = slice(c * BANK, (c + 1) * BANK)
+                    nc.tensor.matmul_mx(
+                        out=banks[c][:],
+                        lhsT=w1q[a, b][t][0],
+                        lhsT_scale=w1q[a, b][t][1],
+                        rhs=v_w[a][:, cols].bitcast(FP8X4),
+                        rhs_scale=v_sc[4 * a : P, cols],
+                        start=(a == 0),
+                        stop=(a == PASSES - 1),
+                    )
+            h = keep.tile([P, S], F32, name=f"h_{b}_{t}")
+            nc.scalar.copy(out=h[:, 0:BANK], in_=banks[0][:])
+            if (b, t) == (0, 0):
+                nc.vector.tensor_copy(out=h[:, BANK:S], in_=banks[1][:])
+            else:
+                nc.scalar.copy(out=h[:, BANK:S], in_=banks[1][:])
+            h_sb[b, t] = h
+
+        def pick_second(second, b, t, cols):
+            nc.vector.tensor_copy(second, h_sb[b, t][:].indirect(pos2_sb[:, cols.start // 16 : cols.stop // 16]))
+
+        def difference(x, second, b, t, cols):
+            nc.vector.tensor_tensor(
+                x, h_sb[b, t][:].indirect(pos1_sb[:, cols.start // 16 : cols.stop // 16]), second, ALU.subtract
+            )
+
+        def differences_by_halves(x, second, b, t, cols):
+            n = (cols.stop - cols.start) // 2
+            parts = [(slice(k * n, (k + 1) * n), slice(cols.start + k * n, cols.start + (k + 1) * n)) for k in range(2)]
+            for here, lines in parts:
+                pick_second(second[:, here], b, t, lines)
+            for here, lines in parts:
+                difference(x[:, t, here], second[:, here], b, t, lines)
+
+        def quantize_x(x, a, cols, weave, tag, bufs):
+            woven = ring.tile([P, x.shape[2] * PACK], BF16, name="woven", tag=tag, bufs=bufs, align_bytes=64)
+            weave(
+                out=woven[:].rearrange("p (c i t) -> p c t i", i=4, t=PACK),
+                in_=x[:].rearrange("p t (c i) -> p c t i", i=4),
+            )
+            nc.vector.quantize_mx(out=x_ops[a][0][:, cols].bitcast(FP8X4), scales=x_ops[a][1][:, cols], in_=woven[:])
+
+        def scaled_own(b, t):
+            own = ring.tile([P, S], F32, name="own", bufs=4)
+            nc.scalar.activation(out=own[:], in_=h_sb[b, t][:], func=ACT.Copy, scale=gain_sb[:, b, t : t + 1])
+            return own
+
+        x_ops = [
+            (
+                keep.tile([P, L], U32, name=f"x{a}_codes", align_bytes=64),
+                keep.tile([P, L], U8, name=f"x{a}_scales", align_bytes=64),
+            )
+            for a in range(PASSES)
+        ]
+
+        whole = slice(0, L)
+        x0 = ring.tile([P, PACK, L], F32, name="x0", tag="wide", align_bytes=64)
+
+        def differences0(t, tag="second0", bufs=2):
+            second0 = ring.tile([P, L], F32, name="second0", tag=tag, bufs=bufs, align_bytes=64)
+            differences_by_halves(x0, second0[:], 0, t, whole)
+
+        first_stage(0, 0)
+        first_stage(0, 1)
+        w1q[1, 0].extend(weight_operands(w1_raw[1, 0], "w1_10", 2, 4))
+        differences0(0)
+        w1q[0, 1] = weight_operands(w1_raw[0, 1], "w1_01", 0, 2)
+        w1q[1, 1] = weight_operands(w1_raw[1, 1], "w1_11", 0, 2, tag="mid_x0", bufs=1)
+        differences0(1)
+        first_stage(0, 2)
+        first_stage(0, 3)
+        differences0(2, "mid_x0", 1)
+        differences0(3)
+        w1q[0, 1].extend(weight_operands(w1_raw[0, 1], "w1_01", 2, 4))
+        w1q[1, 1].extend(weight_operands(w1_raw[1, 1], "w1_11", 2, 4, tag="before_x0", bufs=1))
+        first_stage(1, 0)
+        first_stage(1, 1)
+        wdq = {}
+        for a in range(PASSES):
+            wdq[a, 0] = weight_operands(wd_raw[a, 0], f"wd_{a}0", 0, 2)
+        owns = {(0, t): scaled_own(0, t) for t in range(2)}
+        first_stage(1, 2)
+        first_stage(1, 3)
+        quantize_x(x0, 0, whole, nc.scalar.copy, "before_x0", 1)
+
+        CHUNKS = [slice(0, 256), slice(256, 384), slice(384, 512)]
+
+        def products(b, t, num, den, cols):
+            n0 = b * KP + t * P
+            for a in range(PASSES):
+                nc.tensor.matmul_mx(
+                    out=den,
+                    lhsT=wdq[a, b][t][0],
+                    lhsT_scale=wdq[a, b][t][1],
+                    rhs=x_ops[a][0][:, cols].bitcast(FP8X4),
+                    rhs_scale=x_ops[a][1][:, cols],
+                    start=(a == 0),
+                    stop=(a == PASSES - 1),
+                )
+            for a in range(PASSES):
+                nc.tensor.matmul_mx(
+                    out=num,
+                    lhsT=wn_w[:, 2 * (a * H + n0) : 2 * (a * H + n0 + P)].bitcast(FP4X4),
+                    lhsT_scale=wn_sc[:, a * H + n0 : a * H + n0 + P],
+                    rhs=x_ops[a][0][:, cols].bitcast(FP8X4),
+                    rhs_scale=x_ops[a][1][:, cols],
+                    start=(a == 0),
+                    stop=(a == PASSES - 1),
+                )
+
+        def damping(b, t, cols):
+            n = cols.stop - cols.start
+            num = psum.tile([P, BANK], F32, name="bank")
+            den = psum.tile([P, BANK], F32, name="bank")
+            products(b, t, num[:, 0:n], den[:, 0:n], cols)
+            if cols in (CHUNKS[0], CHUNKS[-1]):
+                tag = "gate" if cols == CHUNKS[-1] else "last_x"
+                damp = ring.tile([P, n], F32, name="damp", tag=tag, bufs=1, align_bytes=64)
+            else:
+                damp = ring.tile([P, n], F32, name="damp", bufs=3)
+            halves = [slice(0, n // 2), slice(n // 2, n)] if n > P else [slice(0, n)]
+            for half in halves:
+                nc.scalar.activation(out=damp[:, half], in_=den[:, half], func=ACT.Abs, bias=bd_sb[:, b, t : t + 1])
+            for half in halves:
+                nc.scalar.activation(out=damp[:, half], in_=damp[:, half], func=ACT.Abs_reciprocal_sqrt, bias=1.0)
+            for half in halves:
+                nc.scalar.activation(out=damp[:, half], in_=damp[:, half], func=ACT.Square)
+            return num[:, 0:n], damp[:]
+
+        y0 = ring.tile([P, L], F32, name="y")
+        for c, cols in enumerate(CHUNKS):
+            n = cols.stop - cols.start
+            x1 = ring.tile([P, PACK, n], F32, name="x1")
+            second1 = ring.tile(
+                [P, PACK, n], F32, name="second1", tag="second1" if c < 2 else "first_x1", bufs=1, align_bytes=64
+            )
+            if c == 0:
+                for t in range(PACK):
+                    differences_by_halves(x1, second1[:, t, :], 1, t, cols)
+                quantize_x(x1, 1, cols, nc.scalar.copy, "first_x1", 1)
+                wdq[0, 0].extend(weight_operands(wd_raw[0, 0], "wd_00", 2, 4))
+            else:
+                for t in range(PACK):
+                    pick_second(second1[:, t, :], 1, t, cols)
+                for t in range(PACK):
+                    difference(x1[:, t, :], second1[:, t, :], 1, t, cols)
+            if c == 1:
+                quantize_x(x1, 1, cols, nc.scalar.copy, "woven", 3)
+                for t in range(2, PACK):
+                    owns[0, t] = scaled_own(0, t)
+                num, damp = damping(0, 0, CHUNKS[0])
+                nc.vector.tensor_tensor(y0[:, CHUNKS[0]], num, damp, ALU.mult)
+            if c == 2:
+                quantize_x(x1, 1, cols, nc.vector.tensor_copy, "last_x", 1)
+
+        out_rows = out.rearrange("(b p t) j -> b t p j", b=PASSES, t=PACK)
+        for b in range(PASSES):
+            for t in range(PACK):
+                i = PACK * b + t
+                y = y0 if i == 0 else ring.tile([P, L], F32, name="y")
+                for cols in CHUNKS[1:] if i == 0 else [whole]:
+                    num, damp = damping(b, t, cols)
+                    if cols == CHUNKS[-1]:
+                        wdq[1, 0].extend(
+                            weight_operands(wd_raw[1, 0], "wd_10", 2, 4, nc.vector.tensor_copy, "last_x", 1)
+                        )
+                    nc.vector.tensor_tensor(y[:, cols], num, damp, ALU.mult)
+                if b == 1:
+                    owns[b, t] = scaled_own(b, t)
+                if 1 <= i < 5:
+                    a, t0 = (i - 1) % 2, 2 * ((i - 1) // 2)
+                    wdq.setdefault((a, 1), []).extend(
+                        weight_operands(wd_raw[a, 1], f"wd_{a}1", t0, t0 + 2, tag="gate", bufs=1)
+                    )
+                own = owns[b, t]
+                res = ring.tile([P, S], F32, name="res", bufs=3)
+                for j0 in range(0, S, BACK):
+                    nc.vector.tensor_tensor(
+                        res[:, j0 : j0 + BACK],
+                        y[:].indirect(pos3_sb[:, j0 // 16 : (j0 + BACK) // 16]),
+                        own[:, j0 : j0 + BACK],
+                        ALU.add,
+                    )
+                    if (b, t) == (PASSES - 1, PACK - 1):
+                        nc.sync.dma_start(out=out_rows[b, t][:, j0 : j0 + BACK], in_=res[:, j0 : j0 + BACK])
+                if (b, t) != (PASSES - 1, PACK - 1):
+                    nc.sync.dma_start(out=out_rows[b, t], in_=res[:])

@@ -319,14 +319,14 @@ def tile_list_longline_buoy_biomass_kernel(
                     )
                 own = owns[b, t]
                 res = ring.tile([P, S], F32, name="res", bufs=3)
+                last = i == PASSES * PACK - 1
+                step = BACK if last else 2 * BACK
                 for j0 in range(0, S, BACK):
-                    nc.vector.tensor_tensor(
-                        res[:, j0 : j0 + BACK],
-                        y[:].indirect(pos3_sb[:, j0 // 16 : (j0 + BACK) // 16]),
-                        own[:, j0 : j0 + BACK],
-                        ALU.add,
-                    )
-                    if (b, t) == (PASSES - 1, PACK - 1):
-                        nc.sync.dma_start(out=out_rows[b, t][:, j0 : j0 + BACK], in_=res[:, j0 : j0 + BACK])
-                if (b, t) != (PASSES - 1, PACK - 1):
+                    nc.vector.tensor_copy(res[:, j0 : j0 + BACK], y[:].indirect(pos3_sb[:, j0 // 16 : (j0 + BACK) // 16]))
+                    if (j0 + BACK) % step == 0:
+                        part = slice(j0 + BACK - step, j0 + BACK)
+                        nc.gpsimd.tensor_tensor(res[:, part], res[:, part], own[:, part], ALU.add)
+                        if last:
+                            nc.sync.dma_start(out=out_rows[b, t][:, part], in_=res[:, part])
+                if not last:
                     nc.sync.dma_start(out=out_rows[b, t], in_=res[:])

@@ -44,8 +44,8 @@ def tile_list_longline_buoy_biomass_kernel(
         tab_sc = keep.tile([P, T], U8, name="tab_sc", align_bytes=64)
         wn_sc_raw = keep.tile([P, PASSES * H], U8, name="wn_sc_raw", align_bytes=64)
         wn_raw = keep.tile([P, PASSES * 2 * H], U8, name="wn_raw", align_bytes=64)
-        nc.vector.memset(wn_sc_raw[:].bitcast(I32), 0)
-        nc.gpsimd.memset(tab_sc[:].bitcast(I32), 0)
+        nc.vector.memset(tab_sc[:].bitcast(I32), 0)
+        nc.gpsimd.memset(wn_sc_raw[:].bitcast(I32), 0)
 
         def load_weight(w, a, b):
             raw = ring.tile([P, PACK, KP], F32, name="w_raw", bufs=5)
@@ -63,21 +63,19 @@ def tile_list_longline_buoy_biomass_kernel(
             return words
 
         def load_table_scales(a):
-            for q in range(4):
+            for r in range(4):
                 nc.sync.dma_start(
-                    out=tab_sc[32 * q + 4 * a : 32 * q + 4 * a + 4, :].bitcast(I32),
-                    in_=tab_scales[a, 4 * q : 4 * q + 4, :].bitcast(I32),
+                    out=tab_sc[4 * a + r : P : 32, :].bitcast(I32), in_=tab_scales[a, r:16:4, :].bitcast(I32)
                 )
 
         nc.sync.dma_start(
             out=wn_raw[:].bitcast(I32).rearrange("p (a c) -> p a c", a=PASSES),
             in_=wn_words.bitcast(I32).rearrange("a p c -> p a c"),
         )
-        for q in range(4):
-            nc.sync.dma_start(
-                out=wn_sc_raw[32 * q : 32 * q + 4, :].bitcast(I32).rearrange("r (a c) -> r a c", a=PASSES),
-                in_=wn_scales[:, 4 * q : 4 * q + 4, :].bitcast(I32).rearrange("a r c -> r a c"),
-            )
+        nc.sync.dma_start(
+            out=wn_sc_raw[0:16, :].bitcast(I32).rearrange("q (a c) -> q a c", a=PASSES),
+            in_=wn_scales.bitcast(I32).rearrange("a q c -> q a c"),
+        )
         tab_w = [load_table(0)]
         nc.sync.dma_start(offs_sb[:], offs)
         load_table_scales(0)
@@ -116,13 +114,17 @@ def tile_list_longline_buoy_biomass_kernel(
         wn_w = keep.tile([P, PASSES * 2 * H], U8, name="wn_w", align_bytes=64)
         wn_sc = keep.tile([P, PASSES * H], U8, name="wn_sc", align_bytes=64)
         nc.vector.tensor_copy(
-            out=wn_w[:].bitcast(U16).rearrange("p (g t m) -> p g m t", t=PACK, m=P),
-            in_=wn_raw[:].bitcast(U16).rearrange("p (g m t) -> p g m t", t=PACK, m=P),
+            out=wn_w[:].bitcast(U16).rearrange("p (g t m) -> p g t m", t=PACK, m=P),
+            in_=wn_raw[:].bitcast(U16).rearrange("p (g m t) -> p g t m", t=PACK, m=P),
         )
         nc.vector.tensor_copy(
-            out=wn_sc[:].rearrange("p (g t m) -> p g m t", t=PACK, m=P),
-            in_=wn_sc_raw[:].rearrange("p (g m t) -> p g m t", t=PACK, m=P),
+            out=wn_sc[:].rearrange("p (g t m) -> p g t m", t=PACK, m=P),
+            in_=wn_sc_raw[:].rearrange("p (g m t) -> p g t m", t=PACK, m=P),
         )
+        for q in range(1, 4):
+            nc.sync.dma_start(
+                out=wn_sc[32 * q : 32 * q + 4, :].bitcast(I32), in_=wn_sc[4 * q : 4 * q + 4, :].bitcast(I32)
+            )
 
         def pick_words(a):
             picked = keep.tile([P, S], U32, name=f"v_w{a}", align_bytes=64)
@@ -135,7 +137,8 @@ def tile_list_longline_buoy_biomass_kernel(
         w1q = {}
         w1q[0, 0] = weight_operands(w1_raw[0, 0], "w1_00", 0, 2) + weight_operands(w1_raw[0, 0], "w1_00", 2, 4)
         v_w.append(pick_words(1))
-        w1q[1, 0] = weight_operands(w1_raw[1, 0], "w1_10", 0, 2)
+        w1q[1, 0] = weight_operands(w1_raw[1, 0], "w1_10", 0, 2, nc.vector.tensor_copy)
+        w1q[1, 0].extend(weight_operands(w1_raw[1, 0], "w1_10", 2, 4))
 
         h_sb = {}
 
@@ -186,8 +189,11 @@ def tile_list_longline_buoy_biomass_kernel(
             nc.vector.quantize_mx(out=x_ops[a][0][:, cols].bitcast(FP8X4), scales=x_ops[a][1][:, cols], in_=woven[:])
 
         def scaled_own(b, t):
-            own = ring.tile([P, S], F32, name="own", bufs=4)
-            nc.scalar.activation(out=own[:], in_=h_sb[b, t][:], func=ACT.Copy, scale=gain_sb[:, b, t : t + 1])
+            own = ring.tile([P, S], F32, name="own", tag=f"row_tile{t}", bufs=1, align_bytes=64)
+            if b == 0:
+                nc.gpsimd.tensor_scalar(own[:], h_sb[b, t][:], gain_sb[:, b, t : t + 1], 0.0, ALU.mult, ALU.add)
+            else:
+                nc.scalar.activation(out=own[:], in_=h_sb[b, t][:], func=ACT.Copy, scale=gain_sb[:, b, t : t + 1])
             return own
 
         x_ops = [
@@ -201,20 +207,22 @@ def tile_list_longline_buoy_biomass_kernel(
         whole = slice(0, L)
         x0 = ring.tile([P, PACK, L], F32, name="x0", tag="wide", align_bytes=64)
 
-        def differences0(t, tag="second0", bufs=2):
-            second0 = ring.tile([P, L], F32, name="second0", tag=tag, bufs=bufs, align_bytes=64)
+        owns = {}
+
+        def differences0(t):
+            second0 = ring.tile([P, L], F32, name="second0", tag=f"row_tile{t}", bufs=1, align_bytes=64)
             differences_by_halves(x0, second0[:], 0, t, whole)
+            owns[0, t] = scaled_own(0, t)
 
         first_stage(0, 0)
         first_stage(0, 1)
-        w1q[1, 0].extend(weight_operands(w1_raw[1, 0], "w1_10", 2, 4))
         differences0(0)
         w1q[0, 1] = weight_operands(w1_raw[0, 1], "w1_01", 0, 2)
-        w1q[1, 1] = weight_operands(w1_raw[1, 1], "w1_11", 0, 2, tag="mid_x0", bufs=1)
+        w1q[1, 1] = weight_operands(w1_raw[1, 1], "w1_11", 0, 2, tag="row_tile2", bufs=1)
         differences0(1)
         first_stage(0, 2)
         first_stage(0, 3)
-        differences0(2, "mid_x0", 1)
+        differences0(2)
         differences0(3)
         w1q[0, 1].extend(weight_operands(w1_raw[0, 1], "w1_01", 2, 4))
         w1q[1, 1].extend(weight_operands(w1_raw[1, 1], "w1_11", 2, 4, tag="before_x0", bufs=1))
@@ -223,7 +231,6 @@ def tile_list_longline_buoy_biomass_kernel(
         wdq = {}
         for a in range(PASSES):
             wdq[a, 0] = weight_operands(wd_raw[a, 0], f"wd_{a}0", 0, 2)
-        owns = {(0, t): scaled_own(0, t) for t in range(2)}
         first_stage(1, 2)
         first_stage(1, 3)
         quantize_x(x0, 0, whole, nc.scalar.copy, "before_x0", 1)
@@ -254,25 +261,30 @@ def tile_list_longline_buoy_biomass_kernel(
                 )
 
         def damping(b, t, cols):
+            i = PACK * b + t
             n = cols.stop - cols.start
             num = psum.tile([P, BANK], F32, name="bank")
             den = psum.tile([P, BANK], F32, name="bank")
             products(b, t, num[:, 0:n], den[:, 0:n], cols)
-            if cols in (CHUNKS[0], CHUNKS[-1]):
-                tag = "gate" if cols == CHUNKS[-1] else "last_x"
-                damp = ring.tile([P, n], F32, name="damp", tag=tag, bufs=1, align_bytes=64)
+            if i == 0:
+                size = ring.tile([P, n], F32, name="size", tag="late1", bufs=1)
+                if cols == CHUNKS[-1]:
+                    root = ring.tile([P, n], F32, name="root", tag="gate", bufs=1, align_bytes=64)
+                else:
+                    root = ring.tile([P, n], F32, name="root")
+                damp = root
             else:
-                damp = ring.tile([P, n], F32, name="damp", bufs=3)
+                size = root = ring.tile([P, n], F32, name="root", tag=f"late{i % 3}", bufs=1)
+                damp = ring.tile([P, n], F32, name="damp")
             halves = [slice(0, n // 2), slice(n // 2, n)] if n > P else [slice(0, n)]
             for half in halves:
-                nc.scalar.activation(out=damp[:, half], in_=den[:, half], func=ACT.Abs, bias=bd_sb[:, b, t : t + 1])
+                nc.scalar.activation(out=size[:, half], in_=den[:, half], func=ACT.Abs, bias=bd_sb[:, b, t : t + 1])
             for half in halves:
-                nc.scalar.activation(out=damp[:, half], in_=damp[:, half], func=ACT.Abs_reciprocal_sqrt, bias=1.0)
+                nc.scalar.activation(out=root[:, half], in_=size[:, half], func=ACT.Abs_reciprocal_sqrt, bias=1.0)
             for half in halves:
-                nc.scalar.activation(out=damp[:, half], in_=damp[:, half], func=ACT.Square)
+                nc.scalar.activation(out=damp[:, half], in_=root[:, half], func=ACT.Square)
             return num[:, 0:n], damp[:]
 
-        y0 = ring.tile([P, L], F32, name="y")
         for c, cols in enumerate(CHUNKS):
             n = cols.stop - cols.start
             x1 = ring.tile([P, PACK, n], F32, name="x1")
@@ -289,27 +301,38 @@ def tile_list_longline_buoy_biomass_kernel(
                     pick_second(second1[:, t, :], 1, t, cols)
                 for t in range(PACK):
                     difference(x1[:, t, :], second1[:, t, :], 1, t, cols)
-            if c == 1:
-                quantize_x(x1, 1, cols, nc.scalar.copy, "woven", 3)
-                for t in range(2, PACK):
-                    owns[0, t] = scaled_own(0, t)
-                num, damp = damping(0, 0, CHUNKS[0])
-                nc.vector.tensor_tensor(y0[:, CHUNKS[0]], num, damp, ALU.mult)
-            if c == 2:
-                quantize_x(x1, 1, cols, nc.vector.tensor_copy, "last_x", 1)
+                quantize_x(x1, 1, cols, nc.scalar.copy if c == 1 else nc.vector.tensor_copy, "last_x", 1)
 
         out_rows = out.rearrange("(b p t) j -> b t p j", b=PASSES, t=PACK)
+
+        def send_back(res, y, b, t, j0):
+            nc.vector.tensor_tensor(
+                res,
+                y[:].indirect(pos3_sb[:, j0 // 16 : (j0 + BACK) // 16]),
+                owns[b, t][:, j0 : j0 + BACK],
+                ALU.add,
+            )
+
+        def last_slice(y, b, t):
+            res = ring.tile([P, BACK], F32, name="res_last", tag=f"late{(PACK * b + t + 1) % 3}", bufs=1)
+            send_back(res[:], y, b, t, S - BACK)
+            nc.sync.dma_start(out=out_rows[b, t][:, S - BACK : S], in_=res[:])
+
+        previous = None
         for b in range(PASSES):
             for t in range(PACK):
                 i = PACK * b + t
-                y = y0 if i == 0 else ring.tile([P, L], F32, name="y")
-                for cols in CHUNKS[1:] if i == 0 else [whole]:
+                y = ring.tile([P, L], F32, name="y")
+                for cols in CHUNKS if i == 0 else [whole]:
                     num, damp = damping(b, t, cols)
                     if cols == CHUNKS[-1]:
                         wdq[1, 0].extend(
                             weight_operands(wd_raw[1, 0], "wd_10", 2, 4, nc.vector.tensor_copy, "last_x", 1)
                         )
                     nc.vector.tensor_tensor(y[:, cols], num, damp, ALU.mult)
+                if previous is not None:
+                    last_slice(*previous)
+                previous = (y, b, t)
                 if b == 1:
                     owns[b, t] = scaled_own(b, t)
                 if 1 <= i < 5:
@@ -317,16 +340,12 @@ def tile_list_longline_buoy_biomass_kernel(
                     wdq.setdefault((a, 1), []).extend(
                         weight_operands(wd_raw[a, 1], f"wd_{a}1", t0, t0 + 2, tag="gate", bufs=1)
                     )
-                own = owns[b, t]
-                res = ring.tile([P, S], F32, name="res", bufs=3)
+                res = ring.tile([P, S - BACK], F32, name="res", bufs=3)
                 last = i == PASSES * PACK - 1
-                step = BACK if last else 2 * BACK
-                for j0 in range(0, S, BACK):
-                    nc.vector.tensor_copy(res[:, j0 : j0 + BACK], y[:].indirect(pos3_sb[:, j0 // 16 : (j0 + BACK) // 16]))
-                    if (j0 + BACK) % step == 0:
-                        part = slice(j0 + BACK - step, j0 + BACK)
-                        nc.gpsimd.tensor_tensor(res[:, part], res[:, part], own[:, part], ALU.add)
-                        if last:
-                            nc.sync.dma_start(out=out_rows[b, t][:, part], in_=res[:, part])
+                for j0 in range(0, S - BACK, BACK):
+                    send_back(res[:, j0 : j0 + BACK], y, b, t, j0)
+                    if last:
+                        nc.sync.dma_start(out=out_rows[b, t][:, j0 : j0 + BACK], in_=res[:, j0 : j0 + BACK])
                 if not last:
-                    nc.sync.dma_start(out=out_rows[b, t], in_=res[:])
+                    nc.sync.dma_start(out=out_rows[b, t][:, 0 : S - BACK], in_=res[:])
+        last_slice(*previous)

@@ -20,9 +20,20 @@ P = 128
 PACK = 4
 KP = P * PACK
 PASSES = 2
+ROW_TILES = PASSES * PACK
+SCALE_ROWS = KP // 32
+QUADRANT = 32
 BANK = 512
-HALF = L // 2
-BACK = 256
+PER_COLUMN = 16
+BACK = L // 2
+FIRST_PAIR, SECOND_PAIR = (0, 2), (2, 4)
+ALL_LINES = slice(0, L)
+CHUNKS = [slice(0, 2 * P), slice(2 * P, 3 * P), slice(3 * P, L)]
+TURNS = 3
+
+
+def entries(offsets, part):
+    return offsets[:, part.start // PER_COLUMN : part.stop // PER_COLUMN]
 
 
 def tile_list_longline_buoy_biomass_kernel(
@@ -34,10 +45,10 @@ def tile_list_longline_buoy_biomass_kernel(
         ring = ctx.enter_context(tc.tile_pool(name="ring", bufs=2))
         psum = ctx.enter_context(tc.psum_pool(name="psum", bufs=8))
 
-        offs_sb = keep.tile([P, S // 16], U16, name="offs_sb")
-        pos1_sb = keep.tile([P, L // 16], U16, name="pos1_sb")
-        pos2_sb = keep.tile([P, L // 16], U16, name="pos2_sb")
-        pos3_sb = keep.tile([P, S // 16], U16, name="pos3_sb")
+        offs_sb = keep.tile([P, S // PER_COLUMN], U16, name="offs_sb")
+        pos1_sb = keep.tile([P, L // PER_COLUMN], U16, name="pos1_sb")
+        pos2_sb = keep.tile([P, L // PER_COLUMN], U16, name="pos2_sb")
+        pos3_sb = keep.tile([P, S // PER_COLUMN], U16, name="pos3_sb")
         bd_sb = keep.tile([P, PASSES, PACK], F32, name="bd_sb")
         gain_sb = keep.tile([P, PASSES, PACK], F32, name="gain_sb")
 
@@ -62,25 +73,26 @@ def tile_list_longline_buoy_biomass_kernel(
             )
             return words
 
-        def load_table_scales(a):
-            for r in range(4):
-                nc.sync.dma_start(
-                    out=tab_sc[4 * a + r : P : 32, :].bitcast(I32), in_=tab_scales[a, r:16:4, :].bitcast(I32)
-                )
+        def load_table_scales(half):
+            for r in (2 * half, 2 * half + 1):
+                for a in range(PASSES):
+                    nc.sync.dma_start(
+                        out=tab_sc[4 * a + r : P : QUADRANT, :].bitcast(I32),
+                        in_=tab_scales[a, r:SCALE_ROWS:4, :].bitcast(I32),
+                    )
 
         nc.sync.dma_start(
             out=wn_raw[:].bitcast(I32).rearrange("p (a c) -> p a c", a=PASSES),
             in_=wn_words.bitcast(I32).rearrange("a p c -> p a c"),
         )
         nc.sync.dma_start(
-            out=wn_sc_raw[0:16, :].bitcast(I32).rearrange("q (a c) -> q a c", a=PASSES),
+            out=wn_sc_raw[0:SCALE_ROWS, :].bitcast(I32).rearrange("q (a c) -> q a c", a=PASSES),
             in_=wn_scales.bitcast(I32).rearrange("a q c -> q a c"),
         )
         tab_w = [load_table(0)]
         nc.sync.dma_start(offs_sb[:], offs)
         load_table_scales(0)
-        w1_raw = {}
-        w1_raw[0, 0] = load_weight(w1, 0, 0)
+        w1_raw = {(0, 0): load_weight(w1, 0, 0)}
         load_table_scales(1)
         tab_w.append(load_table(1))
         w1_raw[1, 0] = load_weight(w1, 1, 0)
@@ -93,20 +105,16 @@ def tile_list_longline_buoy_biomass_kernel(
         nc.sync.dma_start(out=gain_sb[:], in_=gain.rearrange("(b p t) -> p b t", b=PASSES, t=PACK))
         wd_raw = {(a, b): load_weight(wd, a, b) for b in range(PASSES) for a in range(PASSES)}
 
-        def quantize(woven, name):
-            n = woven.shape[1] // PACK
-            codes = keep.tile([P, n], U32, name=name + "_codes", align_bytes=64)
-            scales = keep.tile([P, n], U8, name=name + "_scales", align_bytes=64)
-            nc.vector.quantize_mx(out=codes[:].bitcast(FP8X4), scales=scales[:], in_=woven[:])
-            return codes, scales
-
-        def weight_operands(raw, name, t0, t1, weave=nc.scalar.copy, tag="woven", bufs=3):
+        def weight_operands(raw, name, pair, weave=nc.scalar.copy, tag="woven", bufs=3):
+            t0, t1 = pair
             woven = ring.tile([P, (t1 - t0) * KP], BF16, name="woven", tag=tag, bufs=bufs, align_bytes=64)
             weave(
                 out=woven[:].rearrange("p (t m j) -> p m j t", m=P, j=PACK),
                 in_=raw[:].rearrange("p j (m t) -> p m j t", t=PACK)[:, :, :, t0:t1],
             )
-            codes, scales = quantize(woven, f"{name}_{t0}")
+            codes = keep.tile([P, (t1 - t0) * P], U32, name=f"{name}_{t0}_codes", align_bytes=64)
+            scales = keep.tile([P, (t1 - t0) * P], U8, name=f"{name}_{t0}_scales", align_bytes=64)
+            nc.vector.quantize_mx(out=codes[:].bitcast(FP8X4), scales=scales[:], in_=woven[:])
             return [
                 (codes[:, t * P : (t + 1) * P].bitcast(FP8X4), scales[:, t * P : (t + 1) * P]) for t in range(t1 - t0)
             ]
@@ -121,9 +129,10 @@ def tile_list_longline_buoy_biomass_kernel(
             out=wn_sc[:].rearrange("p (g t m) -> p g t m", t=PACK, m=P),
             in_=wn_sc_raw[:].rearrange("p (g m t) -> p g t m", t=PACK, m=P),
         )
-        for q in range(1, 4):
+        for quad in range(1, P // QUADRANT):
             nc.sync.dma_start(
-                out=wn_sc[32 * q : 32 * q + 4, :].bitcast(I32), in_=wn_sc[4 * q : 4 * q + 4, :].bitcast(I32)
+                out=wn_sc[QUADRANT * quad : QUADRANT * quad + 4, :].bitcast(I32),
+                in_=wn_sc[4 * quad : 4 * quad + 4, :].bitcast(I32),
             )
 
         def pick_words(a):
@@ -134,11 +143,11 @@ def tile_list_longline_buoy_biomass_kernel(
         v_w = [pick_words(0)]
         v_sc = keep.tile([P, S], U8, name="v_sc", align_bytes=64)
         nc.vector.tensor_copy(v_sc[:], tab_sc[:].indirect(offs_sb[:]))
-        w1q = {}
-        w1q[0, 0] = weight_operands(w1_raw[0, 0], "w1_00", 0, 2) + weight_operands(w1_raw[0, 0], "w1_00", 2, 4)
+        w1q = {(0, 0): weight_operands(w1_raw[0, 0], "w1_00", FIRST_PAIR)}
+        w1q[0, 0].extend(weight_operands(w1_raw[0, 0], "w1_00", SECOND_PAIR))
         v_w.append(pick_words(1))
-        w1q[1, 0] = weight_operands(w1_raw[1, 0], "w1_10", 0, 2, nc.vector.tensor_copy)
-        w1q[1, 0].extend(weight_operands(w1_raw[1, 0], "w1_10", 2, 4))
+        w1q[1, 0] = weight_operands(w1_raw[1, 0], "w1_10", FIRST_PAIR, nc.vector.tensor_copy)
+        w1q[1, 0].extend(weight_operands(w1_raw[1, 0], "w1_10", SECOND_PAIR))
 
         h_sb = {}
 
@@ -158,35 +167,33 @@ def tile_list_longline_buoy_biomass_kernel(
                     )
             h = keep.tile([P, S], F32, name=f"h_{b}_{t}")
             nc.scalar.copy(out=h[:, 0:BANK], in_=banks[0][:])
-            if (b, t) == (0, 0):
-                nc.vector.tensor_copy(out=h[:, BANK:S], in_=banks[1][:])
-            else:
-                nc.scalar.copy(out=h[:, BANK:S], in_=banks[1][:])
+            empty = nc.vector.tensor_copy if (b, t) == (0, 0) else nc.scalar.copy
+            empty(out=h[:, BANK:S], in_=banks[1][:])
             h_sb[b, t] = h
 
-        def pick_second(second, b, t, cols):
-            nc.vector.tensor_copy(second, h_sb[b, t][:].indirect(pos2_sb[:, cols.start // 16 : cols.stop // 16]))
+        def pick_second(second, b, t, lines):
+            nc.vector.tensor_copy(second, h_sb[b, t][:].indirect(entries(pos2_sb, lines)))
 
-        def difference(x, second, b, t, cols):
-            nc.vector.tensor_tensor(
-                x, h_sb[b, t][:].indirect(pos1_sb[:, cols.start // 16 : cols.stop // 16]), second, ALU.subtract
-            )
+        def difference(x, second, b, t, lines):
+            nc.vector.tensor_tensor(x, h_sb[b, t][:].indirect(entries(pos1_sb, lines)), second, ALU.subtract)
 
-        def differences_by_halves(x, second, b, t, cols):
-            n = (cols.stop - cols.start) // 2
-            parts = [(slice(k * n, (k + 1) * n), slice(cols.start + k * n, cols.start + (k + 1) * n)) for k in range(2)]
-            for here, lines in parts:
-                pick_second(second[:, here], b, t, lines)
-            for here, lines in parts:
-                difference(x[:, t, here], second[:, here], b, t, lines)
+        def differences_by_halves(x, second, b, t, lines):
+            n = (lines.stop - lines.start) // 2
+            halves = [
+                (slice(k * n, (k + 1) * n), slice(lines.start + k * n, lines.start + (k + 1) * n)) for k in range(2)
+            ]
+            for here, part in halves:
+                pick_second(second[:, here], b, t, part)
+            for here, part in halves:
+                difference(x[:, t, here], second[:, here], b, t, part)
 
-        def quantize_x(x, a, cols, weave, tag, bufs):
-            woven = ring.tile([P, x.shape[2] * PACK], BF16, name="woven", tag=tag, bufs=bufs, align_bytes=64)
+        def quantize_x(x, a, lines, weave, tag):
+            woven = ring.tile([P, x.shape[2] * PACK], BF16, name="woven", tag=tag, bufs=1, align_bytes=64)
             weave(
                 out=woven[:].rearrange("p (c i t) -> p c t i", i=4, t=PACK),
                 in_=x[:].rearrange("p t (c i) -> p c t i", i=4),
             )
-            nc.vector.quantize_mx(out=x_ops[a][0][:, cols].bitcast(FP8X4), scales=x_ops[a][1][:, cols], in_=woven[:])
+            nc.vector.quantize_mx(out=xq[a][0][:, lines].bitcast(FP8X4), scales=xq[a][1][:, lines], in_=woven[:])
 
         def scaled_own(b, t):
             own = ring.tile([P, S], F32, name="own", tag=f"row_tile{t}", bufs=1, align_bytes=64)
@@ -196,7 +203,7 @@ def tile_list_longline_buoy_biomass_kernel(
                 nc.scalar.activation(out=own[:], in_=h_sb[b, t][:], func=ACT.Copy, scale=gain_sb[:, b, t : t + 1])
             return own
 
-        x_ops = [
+        xq = [
             (
                 keep.tile([P, L], U32, name=f"x{a}_codes", align_bytes=64),
                 keep.tile([P, L], U8, name=f"x{a}_scales", align_bytes=64),
@@ -204,144 +211,132 @@ def tile_list_longline_buoy_biomass_kernel(
             for a in range(PASSES)
         ]
 
-        whole = slice(0, L)
         x0 = ring.tile([P, PACK, L], F32, name="x0", tag="wide", align_bytes=64)
-
         owns = {}
 
         def differences0(t):
             second0 = ring.tile([P, L], F32, name="second0", tag=f"row_tile{t}", bufs=1, align_bytes=64)
-            differences_by_halves(x0, second0[:], 0, t, whole)
+            differences_by_halves(x0, second0[:], 0, t, ALL_LINES)
             owns[0, t] = scaled_own(0, t)
 
         first_stage(0, 0)
         first_stage(0, 1)
         differences0(0)
-        w1q[0, 1] = weight_operands(w1_raw[0, 1], "w1_01", 0, 2)
-        w1q[1, 1] = weight_operands(w1_raw[1, 1], "w1_11", 0, 2, tag="row_tile2", bufs=1)
+        w1q[0, 1] = weight_operands(w1_raw[0, 1], "w1_01", FIRST_PAIR)
+        w1q[1, 1] = weight_operands(w1_raw[1, 1], "w1_11", FIRST_PAIR, tag="row_tile2", bufs=1)
         differences0(1)
         first_stage(0, 2)
         first_stage(0, 3)
         differences0(2)
         differences0(3)
-        w1q[0, 1].extend(weight_operands(w1_raw[0, 1], "w1_01", 2, 4))
-        w1q[1, 1].extend(weight_operands(w1_raw[1, 1], "w1_11", 2, 4, tag="before_x0", bufs=1))
+        w1q[0, 1].extend(weight_operands(w1_raw[0, 1], "w1_01", SECOND_PAIR))
+        w1q[1, 1].extend(weight_operands(w1_raw[1, 1], "w1_11", SECOND_PAIR, tag="before_x0", bufs=1))
         first_stage(1, 0)
         first_stage(1, 1)
-        wdq = {}
-        for a in range(PASSES):
-            wdq[a, 0] = weight_operands(wd_raw[a, 0], f"wd_{a}0", 0, 2)
+        wdq = {(a, 0): weight_operands(wd_raw[a, 0], f"wd_{a}0", FIRST_PAIR) for a in range(PASSES)}
         first_stage(1, 2)
         first_stage(1, 3)
-        quantize_x(x0, 0, whole, nc.scalar.copy, "before_x0", 1)
+        quantize_x(x0, 0, ALL_LINES, nc.scalar.copy, "before_x0")
 
-        CHUNKS = [slice(0, 256), slice(256, 384), slice(384, 512)]
-
-        def products(b, t, num, den, cols):
-            n0 = b * KP + t * P
-            for a in range(PASSES):
-                nc.tensor.matmul_mx(
-                    out=den,
-                    lhsT=wdq[a, b][t][0],
-                    lhsT_scale=wdq[a, b][t][1],
-                    rhs=x_ops[a][0][:, cols].bitcast(FP8X4),
-                    rhs_scale=x_ops[a][1][:, cols],
-                    start=(a == 0),
-                    stop=(a == PASSES - 1),
-                )
-            for a in range(PASSES):
-                nc.tensor.matmul_mx(
-                    out=num,
-                    lhsT=wn_w[:, 2 * (a * H + n0) : 2 * (a * H + n0 + P)].bitcast(FP4X4),
-                    lhsT_scale=wn_sc[:, a * H + n0 : a * H + n0 + P],
-                    rhs=x_ops[a][0][:, cols].bitcast(FP8X4),
-                    rhs_scale=x_ops[a][1][:, cols],
-                    start=(a == 0),
-                    stop=(a == PASSES - 1),
-                )
-
-        def damping(b, t, cols):
+        def damping(b, t, lines):
             i = PACK * b + t
-            n = cols.stop - cols.start
+            n = lines.stop - lines.start
+            n0 = b * KP + t * P
             num = psum.tile([P, BANK], F32, name="bank")
             den = psum.tile([P, BANK], F32, name="bank")
-            products(b, t, num[:, 0:n], den[:, 0:n], cols)
+            for a in range(PASSES):
+                nc.tensor.matmul_mx(
+                    out=den[:, 0:n],
+                    lhsT=wdq[a, b][t][0],
+                    lhsT_scale=wdq[a, b][t][1],
+                    rhs=xq[a][0][:, lines].bitcast(FP8X4),
+                    rhs_scale=xq[a][1][:, lines],
+                    start=(a == 0),
+                    stop=(a == PASSES - 1),
+                )
+            for a in range(PASSES):
+                nc.tensor.matmul_mx(
+                    out=num[:, 0:n],
+                    lhsT=wn_w[:, 2 * (a * H + n0) : 2 * (a * H + n0 + P)].bitcast(FP4X4),
+                    lhsT_scale=wn_sc[:, a * H + n0 : a * H + n0 + P],
+                    rhs=xq[a][0][:, lines].bitcast(FP8X4),
+                    rhs_scale=xq[a][1][:, lines],
+                    start=(a == 0),
+                    stop=(a == PASSES - 1),
+                )
             if i == 0:
-                size = ring.tile([P, n], F32, name="size", tag="late1", bufs=1)
-                if cols == CHUNKS[-1]:
-                    root = ring.tile([P, n], F32, name="root", tag="gate", bufs=1, align_bytes=64)
+                size = ring.tile([P, n], F32, name="size", tag="turn1", bufs=1)
+                if lines == CHUNKS[-1]:
+                    root = ring.tile([P, n], F32, name="root", tag="after_y0", bufs=1, align_bytes=64)
                 else:
                     root = ring.tile([P, n], F32, name="root")
                 damp = root
             else:
-                size = root = ring.tile([P, n], F32, name="root", tag=f"late{i % 3}", bufs=1)
+                size = root = ring.tile([P, n], F32, name="root", tag=f"turn{i % TURNS}", bufs=1)
                 damp = ring.tile([P, n], F32, name="damp")
-            halves = [slice(0, n // 2), slice(n // 2, n)] if n > P else [slice(0, n)]
-            for half in halves:
-                nc.scalar.activation(out=size[:, half], in_=den[:, half], func=ACT.Abs, bias=bd_sb[:, b, t : t + 1])
-            for half in halves:
-                nc.scalar.activation(out=root[:, half], in_=size[:, half], func=ACT.Abs_reciprocal_sqrt, bias=1.0)
-            for half in halves:
-                nc.scalar.activation(out=damp[:, half], in_=root[:, half], func=ACT.Square)
+            parts = [slice(0, n // 2), slice(n // 2, n)] if n > P else [slice(0, n)]
+            for part in parts:
+                nc.scalar.activation(out=size[:, part], in_=den[:, part], func=ACT.Abs, bias=bd_sb[:, b, t : t + 1])
+            for part in parts:
+                nc.scalar.activation(out=root[:, part], in_=size[:, part], func=ACT.Abs_reciprocal_sqrt, bias=1.0)
+            for part in parts:
+                nc.scalar.activation(out=damp[:, part], in_=root[:, part], func=ACT.Square)
             return num[:, 0:n], damp[:]
 
-        for c, cols in enumerate(CHUNKS):
-            n = cols.stop - cols.start
+        for c, lines in enumerate(CHUNKS):
+            n = lines.stop - lines.start
             x1 = ring.tile([P, PACK, n], F32, name="x1")
             second1 = ring.tile(
                 [P, PACK, n], F32, name="second1", tag="second1" if c < 2 else "first_x1", bufs=1, align_bytes=64
             )
             if c == 0:
                 for t in range(PACK):
-                    differences_by_halves(x1, second1[:, t, :], 1, t, cols)
-                quantize_x(x1, 1, cols, nc.scalar.copy, "first_x1", 1)
-                wdq[0, 0].extend(weight_operands(wd_raw[0, 0], "wd_00", 2, 4))
+                    differences_by_halves(x1, second1[:, t, :], 1, t, lines)
+                quantize_x(x1, 1, lines, nc.scalar.copy, "first_x1")
+                wdq[0, 0].extend(weight_operands(wd_raw[0, 0], "wd_00", SECOND_PAIR))
             else:
                 for t in range(PACK):
-                    pick_second(second1[:, t, :], 1, t, cols)
+                    pick_second(second1[:, t, :], 1, t, lines)
                 for t in range(PACK):
-                    difference(x1[:, t, :], second1[:, t, :], 1, t, cols)
-                quantize_x(x1, 1, cols, nc.scalar.copy if c == 1 else nc.vector.tensor_copy, "last_x", 1)
+                    difference(x1[:, t, :], second1[:, t, :], 1, t, lines)
+                quantize_x(x1, 1, lines, nc.scalar.copy if c == 1 else nc.vector.tensor_copy, "last_x")
 
         out_rows = out.rearrange("(b p t) j -> b t p j", b=PASSES, t=PACK)
 
         def send_back(res, y, b, t, j0):
-            nc.vector.tensor_tensor(
-                res,
-                y[:].indirect(pos3_sb[:, j0 // 16 : (j0 + BACK) // 16]),
-                owns[b, t][:, j0 : j0 + BACK],
-                ALU.add,
-            )
+            buoys = slice(j0, j0 + BACK)
+            nc.vector.tensor_tensor(res, y[:].indirect(entries(pos3_sb, buoys)), owns[b, t][:, buoys], ALU.add)
 
         def last_slice(y, b, t):
-            res = ring.tile([P, BACK], F32, name="res_last", tag=f"late{(PACK * b + t + 1) % 3}", bufs=1)
+            res = ring.tile([P, BACK], F32, name="res_last", tag=f"turn{(PACK * b + t + 1) % TURNS}", bufs=1)
             send_back(res[:], y, b, t, S - BACK)
             nc.sync.dma_start(out=out_rows[b, t][:, S - BACK : S], in_=res[:])
 
+        wd_left = [(a, pair) for pair in (FIRST_PAIR, SECOND_PAIR) for a in range(PASSES)]
         previous = None
         for b in range(PASSES):
             for t in range(PACK):
                 i = PACK * b + t
                 y = ring.tile([P, L], F32, name="y")
-                for cols in CHUNKS if i == 0 else [whole]:
-                    num, damp = damping(b, t, cols)
-                    if cols == CHUNKS[-1]:
+                for lines in CHUNKS if i == 0 else [ALL_LINES]:
+                    num, damp = damping(b, t, lines)
+                    if lines == CHUNKS[-1]:
                         wdq[1, 0].extend(
-                            weight_operands(wd_raw[1, 0], "wd_10", 2, 4, nc.vector.tensor_copy, "last_x", 1)
+                            weight_operands(wd_raw[1, 0], "wd_10", SECOND_PAIR, nc.vector.tensor_copy, "last_x", 1)
                         )
-                    nc.vector.tensor_tensor(y[:, cols], num, damp, ALU.mult)
+                    nc.vector.tensor_tensor(y[:, lines], num, damp, ALU.mult)
                 if previous is not None:
                     last_slice(*previous)
                 previous = (y, b, t)
                 if b == 1:
                     owns[b, t] = scaled_own(b, t)
-                if 1 <= i < 5:
-                    a, t0 = (i - 1) % 2, 2 * ((i - 1) // 2)
+                if 1 <= i <= len(wd_left):
+                    a, pair = wd_left[i - 1]
                     wdq.setdefault((a, 1), []).extend(
-                        weight_operands(wd_raw[a, 1], f"wd_{a}1", t0, t0 + 2, tag="gate", bufs=1)
+                        weight_operands(wd_raw[a, 1], f"wd_{a}1", pair, tag="after_y0", bufs=1)
                     )
                 res = ring.tile([P, S - BACK], F32, name="res", bufs=3)
-                last = i == PASSES * PACK - 1
+                last = i == ROW_TILES - 1
                 for j0 in range(0, S - BACK, BACK):
                     send_back(res[:, j0 : j0 + BACK], y, b, t, j0)
                     if last:

from contextlib import ExitStack

import concourse.mybir as mybir

K, H, T, S, L = 1024, 1024, 4096, 1024, 512
FLOPS = 2 * K * H * S + 2 * 2 * H * H * L

F32 = mybir.dt.float32
BF16 = mybir.dt.bfloat16
I32 = mybir.dt.int32
U32 = mybir.dt.uint32
U16 = mybir.dt.uint16
U8 = mybir.dt.uint8
FP8X4 = mybir.dt.float8_e4m3fn_x4
FP4X4 = mybir.dt.float4_e2m1fn_x4
ACT = mybir.ActivationFunctionType
ALU = mybir.AluOpType

P = 128
PACK = 4
KP = P * PACK
PASSES = 2
ROW_TILES = PASSES * PACK
SCALE_ROWS = KP // 32
QUADRANT = 32
BANK = 512
PER_COLUMN = 16
BACK = L // 2
FIRST_PAIR, SECOND_PAIR = (0, 2), (2, 4)
ALL_LINES = slice(0, L)
CHUNKS = [slice(0, 2 * P), slice(2 * P, 3 * P), slice(3 * P, L)]
TURNS = 3


def entries(offsets, part):
    return offsets[:, part.start // PER_COLUMN : part.stop // PER_COLUMN]


def tile_list_longline_buoy_biomass_kernel(
    tc, tab_words, tab_scales, offs, pos1, pos2, pos3, w1, wn_words, wn_scales, wd, bd, gain, out
):
    nc = tc.nc
    with ExitStack() as ctx:
        keep = ctx.enter_context(tc.tile_pool(name="keep", bufs=1))
        ring = ctx.enter_context(tc.tile_pool(name="ring", bufs=2))
        psum = ctx.enter_context(tc.psum_pool(name="psum", bufs=8))

        offs_sb = keep.tile([P, S // PER_COLUMN], U16, name="offs_sb")
        pos1_sb = keep.tile([P, L // PER_COLUMN], U16, name="pos1_sb")
        pos2_sb = keep.tile([P, L // PER_COLUMN], U16, name="pos2_sb")
        pos3_sb = keep.tile([P, S // PER_COLUMN], U16, name="pos3_sb")
        bd_sb = keep.tile([P, PASSES, PACK], F32, name="bd_sb")
        gain_sb = keep.tile([P, PASSES, PACK], F32, name="gain_sb")

        tab_sc = keep.tile([P, T], U8, name="tab_sc", align_bytes=64)
        wn_sc_raw = keep.tile([P, PASSES * H], U8, name="wn_sc_raw", align_bytes=64)
        wn_raw = keep.tile([P, PASSES * 2 * H], U8, name="wn_raw", align_bytes=64)
        nc.vector.memset(tab_sc[:].bitcast(I32), 0)
        nc.gpsimd.memset(wn_sc_raw[:].bitcast(I32), 0)

        def load_weight(w, a, b):
            raw = ring.tile([P, PACK, KP], F32, name="w_raw", bufs=5)
            nc.sync.dma_start(
                out=raw[:],
                in_=w[a * KP : (a + 1) * KP, b * KP : (b + 1) * KP].rearrange("(p j) c -> p j c", j=PACK),
            )
            return raw

        def load_table(a):
            words = ring.tile([P, T], U32, name="tab_w", tag="wide", align_bytes=64)
            nc.sync.dma_start(
                out=words[:].bitcast(I32), in_=tab_words[a].rearrange("p t i -> p (t i)").bitcast(I32)
            )
            return words

        def load_table_scales(half):
            for r in (2 * half, 2 * half + 1):
                for a in range(PASSES):
                    nc.sync.dma_start(
                        out=tab_sc[4 * a + r : P : QUADRANT, :].bitcast(I32),
                        in_=tab_scales[a, r:SCALE_ROWS:4, :].bitcast(I32),
                    )

        nc.sync.dma_start(
            out=wn_raw[:].bitcast(I32).rearrange("p (a c) -> p a c", a=PASSES),
            in_=wn_words.bitcast(I32).rearrange("a p c -> p a c"),
        )
        nc.sync.dma_start(
            out=wn_sc_raw[0:SCALE_ROWS, :].bitcast(I32).rearrange("q (a c) -> q a c", a=PASSES),
            in_=wn_scales.bitcast(I32).rearrange("a q c -> q a c"),
        )
        tab_w = [load_table(0)]
        nc.sync.dma_start(offs_sb[:], offs)
        load_table_scales(0)
        w1_raw = {(0, 0): load_weight(w1, 0, 0)}
        load_table_scales(1)
        tab_w.append(load_table(1))
        w1_raw[1, 0] = load_weight(w1, 1, 0)
        nc.sync.dma_start(pos2_sb[:], pos2)
        nc.sync.dma_start(pos1_sb[:], pos1)
        for a in range(PASSES):
            w1_raw[a, 1] = load_weight(w1, a, 1)
        nc.sync.dma_start(pos3_sb[:], pos3)
        nc.sync.dma_start(out=bd_sb[:], in_=bd.rearrange("(b p t) -> p b t", b=PASSES, t=PACK))
        nc.sync.dma_start(out=gain_sb[:], in_=gain.rearrange("(b p t) -> p b t", b=PASSES, t=PACK))
        wd_raw = {(a, b): load_weight(wd, a, b) for b in range(PASSES) for a in range(PASSES)}

        def weight_operands(raw, name, pair, weave=nc.scalar.copy, tag="woven", bufs=3):
            t0, t1 = pair
            woven = ring.tile([P, (t1 - t0) * KP], BF16, name="woven", tag=tag, bufs=bufs, align_bytes=64)
            weave(
                out=woven[:].rearrange("p (t m j) -> p m j t", m=P, j=PACK),
                in_=raw[:].rearrange("p j (m t) -> p m j t", t=PACK)[:, :, :, t0:t1],
            )
            codes = keep.tile([P, (t1 - t0) * P], U32, name=f"{name}_{t0}_codes", align_bytes=64)
            scales = keep.tile([P, (t1 - t0) * P], U8, name=f"{name}_{t0}_scales", align_bytes=64)
            nc.vector.quantize_mx(out=codes[:].bitcast(FP8X4), scales=scales[:], in_=woven[:])
            return [
                (codes[:, t * P : (t + 1) * P].bitcast(FP8X4), scales[:, t * P : (t + 1) * P]) for t in range(t1 - t0)
            ]

        wn_w = keep.tile([P, PASSES * 2 * H], U8, name="wn_w", align_bytes=64)
        wn_sc = keep.tile([P, PASSES * H], U8, name="wn_sc", align_bytes=64)
        nc.vector.tensor_copy(
            out=wn_w[:].bitcast(U16).rearrange("p (g t m) -> p g t m", t=PACK, m=P),
            in_=wn_raw[:].bitcast(U16).rearrange("p (g m t) -> p g t m", t=PACK, m=P),
        )
        nc.vector.tensor_copy(
            out=wn_sc[:].rearrange("p (g t m) -> p g t m", t=PACK, m=P),
            in_=wn_sc_raw[:].rearrange("p (g m t) -> p g t m", t=PACK, m=P),
        )
        for quad in range(1, P // QUADRANT):
            nc.sync.dma_start(
                out=wn_sc[QUADRANT * quad : QUADRANT * quad + 4, :].bitcast(I32),
                in_=wn_sc[4 * quad : 4 * quad + 4, :].bitcast(I32),
            )

        def pick_words(a):
            picked = keep.tile([P, S], U32, name=f"v_w{a}", align_bytes=64)
            nc.vector.tensor_copy(picked[:], tab_w[a][:].indirect(offs_sb[:]))
            return picked

        v_w = [pick_words(0)]
        v_sc = keep.tile([P, S], U8, name="v_sc", align_bytes=64)
        nc.vector.tensor_copy(v_sc[:], tab_sc[:].indirect(offs_sb[:]))
        w1q = {(0, 0): weight_operands(w1_raw[0, 0], "w1_00", FIRST_PAIR)}
        w1q[0, 0].extend(weight_operands(w1_raw[0, 0], "w1_00", SECOND_PAIR))
        v_w.append(pick_words(1))
        w1q[1, 0] = weight_operands(w1_raw[1, 0], "w1_10", FIRST_PAIR, nc.vector.tensor_copy)
        w1q[1, 0].extend(weight_operands(w1_raw[1, 0], "w1_10", SECOND_PAIR))

        h_sb = {}

        def first_stage(b, t):
            banks = [psum.tile([P, BANK], F32, name="bank") for c in range(S // BANK)]
            for a in range(PASSES):
                for c in range(S // BANK):
                    cols = slice(c * BANK, (c + 1) * BANK)
                    nc.tensor.matmul_mx(
                        out=banks[c][:],
                        lhsT=w1q[a, b][t][0],
                        lhsT_scale=w1q[a, b][t][1],
                        rhs=v_w[a][:, cols].bitcast(FP8X4),
                        rhs_scale=v_sc[4 * a : P, cols],
                        start=(a == 0),
                        stop=(a == PASSES - 1),
                    )
            h = keep.tile([P, S], F32, name=f"h_{b}_{t}")
            nc.scalar.copy(out=h[:, 0:BANK], in_=banks[0][:])
            empty = nc.vector.tensor_copy if (b, t) == (0, 0) else nc.scalar.copy
            empty(out=h[:, BANK:S], in_=banks[1][:])
            h_sb[b, t] = h

        def pick_second(second, b, t, lines):
            nc.vector.tensor_copy(second, h_sb[b, t][:].indirect(entries(pos2_sb, lines)))

        def difference(x, second, b, t, lines):
            nc.vector.tensor_tensor(x, h_sb[b, t][:].indirect(entries(pos1_sb, lines)), second, ALU.subtract)

        def differences_by_halves(x, second, b, t, lines):
            n = (lines.stop - lines.start) // 2
            halves = [
                (slice(k * n, (k + 1) * n), slice(lines.start + k * n, lines.start + (k + 1) * n)) for k in range(2)
            ]
            for here, part in halves:
                pick_second(second[:, here], b, t, part)
            for here, part in halves:
                difference(x[:, t, here], second[:, here], b, t, part)

        def quantize_x(x, a, lines, weave, tag):
            woven = ring.tile([P, x.shape[2] * PACK], BF16, name="woven", tag=tag, bufs=1, align_bytes=64)
            weave(
                out=woven[:].rearrange("p (c i t) -> p c t i", i=4, t=PACK),
                in_=x[:].rearrange("p t (c i) -> p c t i", i=4),
            )
            nc.vector.quantize_mx(out=xq[a][0][:, lines].bitcast(FP8X4), scales=xq[a][1][:, lines], in_=woven[:])

        def scaled_own(b, t):
            own = ring.tile([P, S], F32, name="own", tag=f"row_tile{t}", bufs=1, align_bytes=64)
            if b == 0:
                nc.gpsimd.tensor_scalar(own[:], h_sb[b, t][:], gain_sb[:, b, t : t + 1], 0.0, ALU.mult, ALU.add)
            else:
                nc.scalar.activation(out=own[:], in_=h_sb[b, t][:], func=ACT.Copy, scale=gain_sb[:, b, t : t + 1])
            return own

        xq = [
            (
                keep.tile([P, L], U32, name=f"x{a}_codes", align_bytes=64),
                keep.tile([P, L], U8, name=f"x{a}_scales", align_bytes=64),
            )
            for a in range(PASSES)
        ]

        x0 = ring.tile([P, PACK, L], F32, name="x0", tag="wide", align_bytes=64)
        owns = {}

        def differences0(t):
            second0 = ring.tile([P, L], F32, name="second0", tag=f"row_tile{t}", bufs=1, align_bytes=64)
            differences_by_halves(x0, second0[:], 0, t, ALL_LINES)
            owns[0, t] = scaled_own(0, t)

        first_stage(0, 0)
        first_stage(0, 1)
        differences0(0)
        w1q[0, 1] = weight_operands(w1_raw[0, 1], "w1_01", FIRST_PAIR)
        w1q[1, 1] = weight_operands(w1_raw[1, 1], "w1_11", FIRST_PAIR, tag="row_tile2", bufs=1)
        differences0(1)
        first_stage(0, 2)
        first_stage(0, 3)
        differences0(2)
        differences0(3)
        w1q[0, 1].extend(weight_operands(w1_raw[0, 1], "w1_01", SECOND_PAIR))
        w1q[1, 1].extend(weight_operands(w1_raw[1, 1], "w1_11", SECOND_PAIR, tag="before_x0", bufs=1))
        first_stage(1, 0)
        first_stage(1, 1)
        wdq = {(a, 0): weight_operands(wd_raw[a, 0], f"wd_{a}0", FIRST_PAIR) for a in range(PASSES)}
        first_stage(1, 2)
        first_stage(1, 3)
        quantize_x(x0, 0, ALL_LINES, nc.scalar.copy, "before_x0")

        def damping(b, t, lines):
            i = PACK * b + t
            n = lines.stop - lines.start
            n0 = b * KP + t * P
            num = psum.tile([P, BANK], F32, name="bank")
            den = psum.tile([P, BANK], F32, name="bank")
            for a in range(PASSES):
                nc.tensor.matmul_mx(
                    out=den[:, 0:n],
                    lhsT=wdq[a, b][t][0],
                    lhsT_scale=wdq[a, b][t][1],
                    rhs=xq[a][0][:, lines].bitcast(FP8X4),
                    rhs_scale=xq[a][1][:, lines],
                    start=(a == 0),
                    stop=(a == PASSES - 1),
                )
            for a in range(PASSES):
                nc.tensor.matmul_mx(
                    out=num[:, 0:n],
                    lhsT=wn_w[:, 2 * (a * H + n0) : 2 * (a * H + n0 + P)].bitcast(FP4X4),
                    lhsT_scale=wn_sc[:, a * H + n0 : a * H + n0 + P],
                    rhs=xq[a][0][:, lines].bitcast(FP8X4),
                    rhs_scale=xq[a][1][:, lines],
                    start=(a == 0),
                    stop=(a == PASSES - 1),
                )
            if i == 0:
                size = ring.tile([P, n], F32, name="size", tag="turn1", bufs=1)
                if lines == CHUNKS[-1]:
                    root = ring.tile([P, n], F32, name="root", tag="after_y0", bufs=1, align_bytes=64)
                else:
                    root = ring.tile([P, n], F32, name="root")
                damp = root
            else:
                size = root = ring.tile([P, n], F32, name="root", tag=f"turn{i % TURNS}", bufs=1)
                damp = ring.tile([P, n], F32, name="damp")
            parts = [slice(0, n // 2), slice(n // 2, n)] if n > P else [slice(0, n)]
            for part in parts:
                nc.scalar.activation(out=size[:, part], in_=den[:, part], func=ACT.Abs, bias=bd_sb[:, b, t : t + 1])
            for part in parts:
                nc.scalar.activation(out=root[:, part], in_=size[:, part], func=ACT.Abs_reciprocal_sqrt, bias=1.0)
            for part in parts:
                nc.scalar.activation(out=damp[:, part], in_=root[:, part], func=ACT.Square)
            return num[:, 0:n], damp[:]

        for c, lines in enumerate(CHUNKS):
            n = lines.stop - lines.start
            x1 = ring.tile([P, PACK, n], F32, name="x1")
            second1 = ring.tile(
                [P, PACK, n], F32, name="second1", tag="second1" if c < 2 else "first_x1", bufs=1, align_bytes=64
            )
            if c == 0:
                for t in range(PACK):
                    differences_by_halves(x1, second1[:, t, :], 1, t, lines)
                quantize_x(x1, 1, lines, nc.scalar.copy, "first_x1")
                wdq[0, 0].extend(weight_operands(wd_raw[0, 0], "wd_00", SECOND_PAIR))
            else:
                for t in range(PACK):
                    pick_second(second1[:, t, :], 1, t, lines)
                for t in range(PACK):
                    difference(x1[:, t, :], second1[:, t, :], 1, t, lines)
                quantize_x(x1, 1, lines, nc.scalar.copy if c == 1 else nc.vector.tensor_copy, "last_x")

        out_rows = out.rearrange("(b p t) j -> b t p j", b=PASSES, t=PACK)

        def send_back(res, y, b, t, j0):
            buoys = slice(j0, j0 + BACK)
            nc.vector.tensor_tensor(res, y[:].indirect(entries(pos3_sb, buoys)), owns[b, t][:, buoys], ALU.add)

        def last_slice(y, b, t):
            res = ring.tile([P, BACK], F32, name="res_last", tag=f"turn{(PACK * b + t + 1) % TURNS}", bufs=1)
            send_back(res[:], y, b, t, S - BACK)
            nc.sync.dma_start(out=out_rows[b, t][:, S - BACK : S], in_=res[:])

        wd_left = [(a, pair) for pair in (FIRST_PAIR, SECOND_PAIR) for a in range(PASSES)]
        previous = None
        for b in range(PASSES):
            for t in range(PACK):
                i = PACK * b + t
                y = ring.tile([P, L], F32, name="y")
                for lines in CHUNKS if i == 0 else [ALL_LINES]:
                    num, damp = damping(b, t, lines)
                    if lines == CHUNKS[-1]:
                        wdq[1, 0].extend(
                            weight_operands(wd_raw[1, 0], "wd_10", SECOND_PAIR, nc.vector.tensor_copy, "last_x", 1)
                        )
                    nc.vector.tensor_tensor(y[:, lines], num, damp, ALU.mult)
                if previous is not None:
                    last_slice(*previous)
                previous = (y, b, t)
                if b == 1:
                    owns[b, t] = scaled_own(b, t)
                if 1 <= i <= len(wd_left):
                    a, pair = wd_left[i - 1]
                    wdq.setdefault((a, 1), []).extend(
                        weight_operands(wd_raw[a, 1], f"wd_{a}1", pair, tag="after_y0", bufs=1)
                    )
                res = ring.tile([P, S - BACK], F32, name="res", bufs=3)
                last = i == ROW_TILES - 1
                for j0 in range(0, S - BACK, BACK):
                    send_back(res[:, j0 : j0 + BACK], y, b, t, j0)
                    if last:
                        nc.sync.dma_start(out=out_rows[b, t][:, j0 : j0 + BACK], in_=res[:, j0 : j0 + BACK])
                if not last:
                    nc.sync.dma_start(out=out_rows[b, t][:, 0 : S - BACK], in_=res[:])
        last_slice(*previous)
